import numpy as np
import ml_dtypes


def mxq(x, axis, fmt="e4m3"):
    dtype, down = {"e4m3": (ml_dtypes.float8_e4m3fn, 7), "e5m2": (ml_dtypes.float8_e5m2, 14)}[fmt]
    v = np.moveaxis(np.asarray(x, np.float32).astype(ml_dtypes.bfloat16).astype(np.float64), axis, -1)
    blocks = v.reshape(v.shape[:-1] + (-1, 32))
    amax = np.abs(blocks).max(-1, keepdims=True)
    byte = np.maximum(np.where(amax > 0, np.frexp(amax)[1] - 1 + 127, 0) - down, 1)
    scale = np.exp2(byte - 127.0)
    codes = (blocks / scale).astype(np.float32).astype(dtype).astype(np.float64)
    return np.moveaxis((codes * scale).reshape(v.shape), -1, axis)


WIDE = False


def mx_kscale(k):
    if not WIDE:
        return np.ones(k)
    levels = np.array([10, -10, 5, -5, 0])
    if k % 512:
        return np.exp2(np.random.permutation(np.resize(levels, k // 32))).repeat(32)
    a = np.empty((k // 512, 16))
    for p in range(k // 512):
        a[p, :8] = np.random.permutation(np.resize(levels, 8))
        for g in range(8):
            far = levels[np.abs(levels - a[p, g]) >= 10]
            a[p, g + 8] = far[np.random.randint(len(far))]
    return np.exp2(a.ravel()).repeat(32)


def f64(x):
    return np.asarray(x).astype(np.float64)


def striped(idx):
    return np.tile(idx.reshape(-1, 16).T, (8, 1)).astype(np.uint16)


def unstriped(offs):
    return offs[:16].T.reshape(-1).astype(np.int64)


def pack_weight(w):
    k, n = w.shape
    w = f64(np.asarray(w, np.float32).astype(ml_dtypes.bfloat16)).reshape(k // 32, 32, n)
    amax = np.abs(w).max(1)
    byte = np.clip(np.where(amax > 0, np.frexp(amax)[1] - 1 + 127 - 7, 1), 1, 254)
    scaled = (w * np.exp2(127.0 - byte)[:, None, :]).reshape(k, n).astype(np.float32)
    words = np.ascontiguousarray(scaled.reshape(k // 512, 128, 4, n).transpose(0, 1, 3, 2)).astype(ml_dtypes.float8_e4m3fn).view(np.uint8)
    return words, np.ascontiguousarray(byte.astype(np.uint8).reshape(k // 512, 16, n))


def unpack_weight(words, scales):
    g, p, n, _ = words.shape
    vals = np.ascontiguousarray(words).view(ml_dtypes.float8_e4m3fn).astype(np.float64) * np.repeat(np.exp2(scales.astype(np.float64) - 127.0), 8, axis=1)[..., None]
    return vals.transpose(0, 1, 3, 2).reshape(g * 512, n)


K, T, S, N, V = 1024, 1024, 512, 128, 256
P = 2 ** 7


def setup_inputs():
    n = np.random.standard_normal
    s = mx_kscale(K)[:, None]
    packed_xT = pack_weight(n((K, T)) * s)
    return {
        "x_words": packed_xT[0],
        "x_scales": packed_xT[1],
        "w1": (n((K, N)) / np.sqrt(K) / s).astype(np.float32),
        "hist": (1.5 * n((N, V))).astype(np.float32),
        "alpha": (np.tile(np.random.uniform(0.1, 0.5, V), (P, 1))).astype(np.float32),
        "offs": striped(np.random.permutation(T)[:S]),
        "pos1": striped(np.random.permutation(S)[:V]),
        "pos2": striped(np.random.permutation(S)[:V]),
        "pos3": striped(np.random.permutation(S)[:V]),
        "pos4": striped(np.random.permutation(S)[:V]),
        "cen": striped(np.random.permutation(S)[:V]),
    }


def reference(x_words, x_scales, w1, hist, alpha, offs, pos1, pos2, pos3, pos4, cen):
    xq = unpack_weight(x_words, x_scales)[:, unstriped(offs)]
    y = mxq(f64(w1), 0, "e4m3").T @ xq
    kw = f64(alpha)[:1] / (np.abs(y[:, unstriped(cen)]) + 1.0)
    g0 = y[:, unstriped(pos1)]
    g1 = y[:, unstriped(pos2)]
    g2 = y[:, unstriped(pos3)]
    g3 = y[:, unstriped(pos4)]
    mu = (g0 + g1 + g2 + g3) / 4
    sd = np.sqrt(((g0 - mu) ** 2 + (g1 - mu) ** 2 + (g2 - mu) ** 2 + (g3 - mu) ** 2) / 4 + 0.01)
    cl = np.maximum(np.minimum(f64(hist), mu + sd), mu - sd)
    kh = (-1.0 * f64(alpha)[:1] + 1.0) / (np.abs(cl) + 1.0)
    return (kw * y[:, unstriped(cen)] + kh * cl) / (kw + kh)

@@ -1,0 +1,215 @@
+import math
+from contextlib import ExitStack
+
+import concourse.mybir as mybir
+from concourse.masks import make_identity
+
+K, T, S, N, V = 1024, 1024, 512, 128, 256
+FLOPS = 2 * K * S * N
+
+F32 = mybir.dt.float32
+BF16 = mybir.dt.bfloat16
+I32 = mybir.dt.int32
+U32 = mybir.dt.uint32
+U16 = mybir.dt.uint16
+U8 = mybir.dt.uint8
+FP8X4 = mybir.dt.float8_e4m3fn_x4
+ALU = mybir.AluOpType
+ACT = mybir.ActivationFunctionType
+
+P = 128
+PACK = 4
+PASSES = K // (P * PACK)
+PER_COL = 16
+PRODUCT_PIECES = [256,128,128]
+BLEND_PIECES = [128,128]
+
+
+def spans(widths):
+    result = []
+    start = 0
+    for width in widths:
+        result.append((start, start + width))
+        start = start + width
+    return result
+
+
+def tile_picked_ytaa_lum_p_kernel(
+    tc, x_words, x_scales, w1, hist, alpha, offs, pos1, pos2, pos3, pos4, cen, out
+):
+    nc = tc.nc
+    with ExitStack() as ctx:
+        sb = ctx.enter_context(tc.tile_pool(name="sb", bufs=1))
+        ps = ctx.enter_context(tc.psum_pool(name="ps", bufs=1))
+
+        def list_tile(name, src):
+            tile = sb.tile([P, src.shape[1]], U16, name=name)
+            nc.sync.dma_start(tile[:], src)
+            return tile
+
+        scale_table = sb.tile([P, T], U8, name="scale_table", align_bytes=64)
+        nc.vector.memset(scale_table[:].bitcast(I32), 0)
+        one_col = sb.tile([P, 1], F32, name="one_col")
+        nc.vector.memset(one_col[:], 1.0)
+
+        offs_sb = list_tile("offs_sb", offs)
+        word_table = [sb.tile([P, T], U32, name=f"word_table{o}", align_bytes=64) for o in range(PASSES)]
+
+        def load_words(o):
+            nc.sync.dma_start(word_table[o][:].bitcast(I32), x_words[o].rearrange("p n t -> p (n t)").bitcast(I32))
+
+        load_words(0)
+        for q in range(4):
+            nc.scalar.dma_start(
+                scale_table[32 * q : 32 * q + 4 * PASSES, :].bitcast(I32),
+                x_scales[:, 4 * q : 4 * q + 4, :].bitcast(I32),
+            )
+        warm = sb.tile([P, 1], F32, name="warm")
+        nc.scalar.activation(warm[:], one_col[:], ACT.Abs_reciprocal_sqrt)
+        w_all = sb.tile([P, PASSES, PACK * N], F32, name="w_all")
+        nc.sync.dma_start(w_all[:], w1.rearrange("(o p j) m -> p o (j m)", o=PASSES, j=PACK))
+        load_words(1)
+        pos_sb = [list_tile(f"pos_sb{i}", src) for i, src in enumerate((pos1, pos2, pos3, pos4))]
+        cen_sb = list_tile("cen_sb", cen)
+        hist_sb = sb.tile([P, V], F32, name="hist_sb")
+        nc.sync.dma_start(hist_sb[:], hist)
+        share = sb.tile([P, 2], F32, name="share")
+        with nc.allow_non_contiguous_dma(reason="one share a partition"):
+            nc.sync.dma_start(share[:], alpha[0].rearrange("(h p) -> p h", p=P))
+        ident = sb.tile([P, P], F32, name="ident")
+        make_identity(nc, ident[:])
+
+        scales = sb.tile([P, S], U8, name="scales", align_bytes=64)
+        nc.vector.tensor_copy(scales[:], scale_table[:].indirect(offs_sb[:]))
+        words = [sb.tile([P, S], U32, name=f"words{o}", align_bytes=64) for o in range(PASSES)]
+        nc.vector.tensor_copy(words[0][:], word_table[0][:].indirect(offs_sb[:]))
+
+        w_codes, w_scales = [], []
+        for o in range(PASSES):
+            w_bf = sb.tile([P, N, PACK], BF16, name=f"w_bf{o}", align_bytes=64)
+            nc.scalar.copy(w_bf[:], w_all[:, o, :].rearrange("p (j m) -> p m j", j=PACK))
+            codes = sb.tile([P, N], U32, name=f"w_codes{o}", align_bytes=64)
+            plane = sb.tile([P, N], U8, name=f"w_scales{o}", align_bytes=64)
+            nc.vector.quantize_mx(
+                out=codes[:].bitcast(FP8X4), scales=plane[:], in_=w_bf[:].rearrange("p m j -> p (m j)")
+            )
+            w_codes.append(codes)
+            w_scales.append(plane)
+
+        acc = [ps.tile([P, b - a], F32, name=f"acc{i}", tag=f"bank{i}") for i, (a, b) in enumerate(spans(PRODUCT_PIECES))]
+
+        def product(o, i, a, b):
+            nc.tensor.matmul_mx(
+                out=acc[i][:],
+                lhsT=w_codes[o][:].bitcast(FP8X4),
+                lhsT_scale=w_scales[o][:],
+                rhs=words[o][:, a:b].bitcast(FP8X4),
+                rhs_scale=scales[4 * o : P, a:b],
+                start=(o == 0),
+                stop=(o == PASSES - 1),
+            )
+
+        for i, (a, b) in enumerate(spans(PRODUCT_PIECES)):
+            product(0, i, a, b)
+        y = sb.tile([P, S], F32, name="y")
+        for i, (a, b) in enumerate(spans(PRODUCT_PIECES)):
+            nc.vector.tensor_copy(
+                words[1][:, a:b], word_table[1][:].indirect(offs_sb[:, a // PER_COL : b // PER_COL])
+            )
+            product(1, i, a, b)
+        for i, (a, b) in enumerate(spans(PRODUCT_PIECES)):
+            if i == len(PRODUCT_PIECES) - 1:
+                nc.vector.tensor_copy(y[:, a:b], acc[i][:])
+            else:
+                nc.scalar.copy(y[:, a:b], acc[i][:])
+
+        sgn01 = sb.tile([P, 2], F32, name="sgn01")
+        nc.gpsimd.tensor_scalar(sgn01[:], share[:], 0.0, 2.0, ALU.is_ge, ALU.mult)
+        sgn = sb.tile([P, 2], F32, name="sgn")
+        nc.gpsimd.tensor_scalar(sgn[:], sgn01[:], 1.0, -1.0, ALU.mult, ALU.add)
+        abs_share = sb.tile([P, 2], F32, name="abs_share")
+        nc.gpsimd.tensor_tensor(abs_share[:], share[:], sgn[:], ALU.mult)
+        keep_s = sb.tile([P, 2], F32, name="keep_s")
+        nc.gpsimd.tensor_tensor(keep_s[:], sgn[:], abs_share[:], ALU.subtract)
+
+        hist_ps = ps.tile([P, 2, P], F32, name="hist_ps", tag="bank7")
+        for h in range(2):
+            nc.tensor.transpose(hist_ps[:, h, :], hist_sb[:, h * P : (h + 1) * P], ident[:])
+        hist_t = sb.tile([P, 2, P], F32, name="hist_t")
+        nc.scalar.copy(hist_t[:], hist_ps[:])
+
+        pieces = spans(BLEND_PIECES)
+        t = [dict() for piece in pieces]
+
+        def new(i, name):
+            t[i][name] = sb.tile([P, P], F32, name=f"{name}{i}")
+            return t[i][name][:]
+
+        def picked(i, lst):
+            a, b = pieces[i]
+            return y[:].indirect(lst[:, a // PER_COL : b // PER_COL])
+
+        def tt(i, name, x, z, op):
+            nc.vector.tensor_tensor(new(i, name), x, z, op)
+
+        def stt(i, name, x, scalar, z, op0, op1):
+            nc.vector.scalar_tensor_tensor(new(i, name), x, scalar, z, op0, op1)
+
+        def act(i, name, x, func, **kw):
+            nc.scalar.activation(new(i, name), x, func, **kw)
+
+        def g(i, name):
+            return t[i][name][:]
+
+        def turn(i, name, bank, x, start, stop):
+            if start:
+                t[i][name] = ps.tile([P, P], F32, name=f"{name}{i}", tag=f"bank{bank + i}")
+            nc.tensor.matmul(t[i][name][:], x, ident[:], start=start, stop=stop, is_transpose=True)
+
+        def col(i, tile):
+            return tile[:, i : i + 1]
+
+        steps = [
+            lambda i: nc.vector.tensor_copy(new(i, "g0"), picked(i, pos_sb[0])),
+            lambda i: tt(i, "u1", picked(i, pos_sb[1]), g(i, "g0"), ALU.subtract),
+            lambda i: stt(i, "m1", g(i, "u1"), 0.5, g(i, "g0"), ALU.mult, ALU.add),
+            lambda i: act(i, "q1", g(i, "u1"), ACT.Square, scale=math.sqrt(1 / 8)),
+            lambda i: tt(i, "u2", picked(i, pos_sb[2]), g(i, "m1"), ALU.subtract),
+            lambda i: turn(i, "Q", 3, g(i, "q1"), True, False),
+            lambda i: stt(i, "m2", g(i, "u2"), 1 / 3, g(i, "m1"), ALU.mult, ALU.add),
+            lambda i: act(i, "q2", g(i, "u2"), ACT.Square, scale=math.sqrt(1 / 6)),
+            lambda i: tt(i, "u3", picked(i, pos_sb[3]), g(i, "m2"), ALU.subtract),
+            lambda i: turn(i, "Q", 3, g(i, "q2"), False, False),
+            lambda i: act(i, "m4", g(i, "m2"), ACT.Copy, scale=4.0),
+            lambda i: act(i, "q3", g(i, "u3"), ACT.Square, scale=math.sqrt(3 / 16)),
+            lambda i: turn(i, "M", 5, g(i, "m4"), True, False),
+            lambda i: turn(i, "M", 5, g(i, "u3"), False, True),
+            lambda i: turn(i, "Q", 3, g(i, "q3"), False, True),
+            lambda i: nc.vector.tensor_copy(new(i, "yc"), picked(i, cen_sb)),
+            lambda i: act(i, "rsd", g(i, "Q"), ACT.Abs_reciprocal_sqrt, bias=0.01),
+            lambda i: turn(i, "Y", 0, g(i, "yc"), True, True),
+            lambda i: stt(i, "hm", g(i, "M"), -0.25, hist_t[:, i, :], ALU.mult, ALU.add),
+            lambda i: stt(i, "sd", g(i, "Q"), 0.01, g(i, "rsd"), ALU.add, ALU.mult),
+            lambda i: act(i, "ay", g(i, "Y"), ACT.Abs),
+            lambda i: tt(i, "t1", g(i, "hm"), g(i, "sd"), ALU.min),
+            lambda i: act(i, "wb", g(i, "ay"), ACT.Identity, scale=col(i, keep_s), bias=col(i, keep_s)),
+            lambda i: turn(i, "D", 3, col(i, abs_share).to_broadcast([P, P]), True, False),
+            lambda i: stt(i, "t2", g(i, "sd"), -1.0, g(i, "t1"), ALU.mult, ALU.max),
+            lambda i: turn(i, "D", 3, g(i, "wb"), False, False),
+            lambda i: stt(i, "cl", g(i, "M"), 0.25, g(i, "t2"), ALU.mult, ALU.add),
+            lambda i: act(i, "ac", g(i, "cl"), ACT.Abs, scale=col(i, share)),
+            lambda i: tt(i, "n2", g(i, "wb"), g(i, "cl"), ALU.mult),
+            lambda i: turn(i, "D", 3, g(i, "ac"), False, True),
+            lambda i: stt(i, "n1", g(i, "ac"), col(i, abs_share), g(i, "Y"), ALU.add, ALU.mult),
+            lambda i: turn(i, "N", 5, g(i, "n2"), True, False),
+            lambda i: act(i, "rd", g(i, "D"), ACT.Abs_reciprocal_sqrt),
+            lambda i: act(i, "sg", g(i, "D"), ACT.Sign),
+            lambda i: turn(i, "N", 5, g(i, "n1"), False, True),
+            lambda i: act(i, "rr", g(i, "rd"), ACT.Square),
+            lambda i: tt(i, "ns", g(i, "N"), g(i, "sg"), ALU.mult),
+            lambda i: tt(i, "res", g(i, "ns"), g(i, "rr"), ALU.mult),
+            lambda i: nc.sync.dma_start(out[:, i * P : (i + 1) * P], g(i, "res")),
+        ]
+        for step in steps:
+            for i in range(len(pieces)):
+                step(i)

@@ -21,17 +21,9 @@ P = 128
 PACK = 4
 PASSES = K // (P * PACK)
 PER_COL = 16
-PRODUCT_PIECES = [256,128,128]
-BLEND_PIECES = [128,128]
-
-
-def spans(widths):
-    result = []
-    start = 0
-    for width in widths:
-        result.append((start, start + width))
-        start = start + width
-    return result
+HALVES = V // P
+BLOCKS = S // P
+LAST_GATHERS = [[0,256],[256,384],[384,512]]
 
 
 def tile_picked_ytaa_lum_p_kernel(
@@ -51,43 +43,57 @@ def tile_picked_ytaa_lum_p_kernel(
         nc.vector.memset(scale_table[:].bitcast(I32), 0)
         one_col = sb.tile([P, 1], F32, name="one_col")
         nc.vector.memset(one_col[:], 1.0)
+        warm = sb.tile([P, 1], F32, name="warm")
+        nc.scalar.activation(warm[:], one_col[:], ACT.Abs_reciprocal_sqrt)
 
-        offs_sb = list_tile("offs_sb", offs)
         word_table = [sb.tile([P, T], U32, name=f"word_table{o}", align_bytes=64) for o in range(PASSES)]
+        w_raw = [sb.tile([P, PACK * N], F32, name=f"w_raw{o}") for o in range(PASSES)]
+        w_rows = w1.rearrange("(o p j) m -> o p (j m)", o=PASSES, j=PACK)
 
         def load_words(o):
             nc.sync.dma_start(word_table[o][:].bitcast(I32), x_words[o].rearrange("p n t -> p (n t)").bitcast(I32))
 
+        def load_scales():
+            for q in range(4):
+                nc.sync.dma_start(
+                    scale_table[32 * q : 32 * q + 4 * PASSES, :].bitcast(I32),
+                    x_scales[:, 4 * q : 4 * q + 4, :].bitcast(I32),
+                )
+
+        offs_sb = list_tile("offs_sb", offs)
         load_words(0)
-        for q in range(4):
-            nc.scalar.dma_start(
-                scale_table[32 * q : 32 * q + 4 * PASSES, :].bitcast(I32),
-                x_scales[:, 4 * q : 4 * q + 4, :].bitcast(I32),
-            )
-        warm = sb.tile([P, 1], F32, name="warm")
-        nc.scalar.activation(warm[:], one_col[:], ACT.Abs_reciprocal_sqrt)
-        w_all = sb.tile([P, PASSES, PACK * N], F32, name="w_all")
-        nc.sync.dma_start(w_all[:], w1.rearrange("(o p j) m -> p o (j m)", o=PASSES, j=PACK))
+        load_scales()
+        nc.sync.dma_start(w_raw[0][:], w_rows[0])
+        nc.sync.dma_start(w_raw[1][:], w_rows[1])
         load_words(1)
+        share = sb.tile([P, HALVES], F32, name="share")
+        with nc.allow_non_contiguous_dma(reason="one share a partition"):
+            nc.sync.dma_start(share[:], alpha[0].rearrange("(h p) -> p h", p=P))
         pos_sb = [list_tile(f"pos_sb{i}", src) for i, src in enumerate((pos1, pos2, pos3, pos4))]
         cen_sb = list_tile("cen_sb", cen)
         hist_sb = sb.tile([P, V], F32, name="hist_sb")
         nc.sync.dma_start(hist_sb[:], hist)
-        share = sb.tile([P, 2], F32, name="share")
-        with nc.allow_non_contiguous_dma(reason="one share a partition"):
-            nc.sync.dma_start(share[:], alpha[0].rearrange("(h p) -> p h", p=P))
         ident = sb.tile([P, P], F32, name="ident")
         make_identity(nc, ident[:])
 
-        scales = sb.tile([P, S], U8, name="scales", align_bytes=64)
-        nc.vector.tensor_copy(scales[:], scale_table[:].indirect(offs_sb[:]))
+        sgn01 = sb.tile([P, HALVES], F32, name="sgn01")
+        nc.gpsimd.tensor_scalar(sgn01[:], share[:], 0.0, 2.0, ALU.is_ge, ALU.mult)
+        sgn = sb.tile([P, HALVES], F32, name="sgn")
+        nc.gpsimd.tensor_scalar(sgn[:], sgn01[:], 1.0, -1.0, ALU.mult, ALU.add)
+        abs_share = sb.tile([P, HALVES], F32, name="abs_share")
+        nc.gpsimd.tensor_tensor(abs_share[:], share[:], sgn[:], ALU.mult)
+        keep_s = sb.tile([P, HALVES], F32, name="keep_s")
+        nc.gpsimd.tensor_tensor(keep_s[:], sgn[:], abs_share[:], ALU.subtract)
+
         words = [sb.tile([P, S], U32, name=f"words{o}", align_bytes=64) for o in range(PASSES)]
         nc.vector.tensor_copy(words[0][:], word_table[0][:].indirect(offs_sb[:]))
+        scales = sb.tile([P, S], U8, name="scales", align_bytes=64)
+        nc.vector.tensor_copy(scales[:], scale_table[:].indirect(offs_sb[:]))
 
         w_codes, w_scales = [], []
         for o in range(PASSES):
             w_bf = sb.tile([P, N, PACK], BF16, name=f"w_bf{o}", align_bytes=64)
-            nc.scalar.copy(w_bf[:], w_all[:, o, :].rearrange("p (j m) -> p m j", j=PACK))
+            nc.scalar.copy(w_bf[:], w_raw[o][:].rearrange("p (j m) -> p m j", j=PACK))
             codes = sb.tile([P, N], U32, name=f"w_codes{o}", align_bytes=64)
             plane = sb.tile([P, N], U8, name=f"w_scales{o}", align_bytes=64)
             nc.vector.quantize_mx(
@@ -96,58 +102,42 @@ def tile_picked_ytaa_lum_p_kernel(
             w_codes.append(codes)
             w_scales.append(plane)
 
-        acc = [ps.tile([P, b - a], F32, name=f"acc{i}", tag=f"bank{i}") for i, (a, b) in enumerate(spans(PRODUCT_PIECES))]
+        acc = [ps.tile([P, P], F32, name=f"acc{i}", tag=f"bank{i}") for i in range(BLOCKS)]
 
-        def product(o, i, a, b):
+        def product(o, i):
             nc.tensor.matmul_mx(
                 out=acc[i][:],
                 lhsT=w_codes[o][:].bitcast(FP8X4),
                 lhsT_scale=w_scales[o][:],
-                rhs=words[o][:, a:b].bitcast(FP8X4),
-                rhs_scale=scales[4 * o : P, a:b],
+                rhs=words[o][:, i * P : (i + 1) * P].bitcast(FP8X4),
+                rhs_scale=scales[4 * o : P, i * P : (i + 1) * P],
                 start=(o == 0),
                 stop=(o == PASSES - 1),
             )
 
-        for i, (a, b) in enumerate(spans(PRODUCT_PIECES)):
-            product(0, i, a, b)
+        for i in range(BLOCKS):
+            product(0, i)
         y = sb.tile([P, S], F32, name="y")
-        for i, (a, b) in enumerate(spans(PRODUCT_PIECES)):
+        for a, b in LAST_GATHERS:
             nc.vector.tensor_copy(
                 words[1][:, a:b], word_table[1][:].indirect(offs_sb[:, a // PER_COL : b // PER_COL])
             )
-            product(1, i, a, b)
-        for i, (a, b) in enumerate(spans(PRODUCT_PIECES)):
-            if i == len(PRODUCT_PIECES) - 1:
-                nc.vector.tensor_copy(y[:, a:b], acc[i][:])
+            for i in range(a // P, b // P):
+                product(1, i)
+        for i in range(BLOCKS):
+            if i == BLOCKS - 1:
+                nc.vector.tensor_scalar(y[:, i * P : (i + 1) * P], acc[i][:], -0.25, None, ALU.mult)
             else:
-                nc.scalar.copy(y[:, a:b], acc[i][:])
+                nc.scalar.activation(y[:, i * P : (i + 1) * P], acc[i][:], ACT.Copy, scale=-0.25)
 
-        sgn01 = sb.tile([P, 2], F32, name="sgn01")
-        nc.gpsimd.tensor_scalar(sgn01[:], share[:], 0.0, 2.0, ALU.is_ge, ALU.mult)
-        sgn = sb.tile([P, 2], F32, name="sgn")
-        nc.gpsimd.tensor_scalar(sgn[:], sgn01[:], 1.0, -1.0, ALU.mult, ALU.add)
-        abs_share = sb.tile([P, 2], F32, name="abs_share")
-        nc.gpsimd.tensor_tensor(abs_share[:], share[:], sgn[:], ALU.mult)
-        keep_s = sb.tile([P, 2], F32, name="keep_s")
-        nc.gpsimd.tensor_tensor(keep_s[:], sgn[:], abs_share[:], ALU.subtract)
+        t = [dict() for h in range(HALVES)]
 
-        hist_ps = ps.tile([P, 2, P], F32, name="hist_ps", tag="bank7")
-        for h in range(2):
-            nc.tensor.transpose(hist_ps[:, h, :], hist_sb[:, h * P : (h + 1) * P], ident[:])
-        hist_t = sb.tile([P, 2, P], F32, name="hist_t")
-        nc.scalar.copy(hist_t[:], hist_ps[:])
-
-        pieces = spans(BLEND_PIECES)
-        t = [dict() for piece in pieces]
-
-        def new(i, name):
-            t[i][name] = sb.tile([P, P], F32, name=f"{name}{i}")
+        def new(i, name, tag=None):
+            t[i][name] = sb.tile([P, P], F32, name=f"{name}{i}", tag=tag or f"{name}{i}")
             return t[i][name][:]
 
         def picked(i, lst):
-            a, b = pieces[i]
-            return y[:].indirect(lst[:, a // PER_COL : b // PER_COL])
+            return y[:].indirect(lst[:, i * P // PER_COL : (i + 1) * P // PER_COL])
 
         def tt(i, name, x, z, op):
             nc.vector.tensor_tensor(new(i, name), x, z, op)
@@ -171,45 +161,50 @@ def tile_picked_ytaa_lum_p_kernel(
 
         steps = [
             lambda i: nc.vector.tensor_copy(new(i, "g0"), picked(i, pos_sb[0])),
+            lambda i: turn(i, "G", 0, hist_sb[:, i * P : (i + 1) * P], True, False),
             lambda i: tt(i, "u1", picked(i, pos_sb[1]), g(i, "g0"), ALU.subtract),
             lambda i: stt(i, "m1", g(i, "u1"), 0.5, g(i, "g0"), ALU.mult, ALU.add),
-            lambda i: act(i, "q1", g(i, "u1"), ACT.Square, scale=math.sqrt(1 / 8)),
+            lambda i: act(i, "q1", g(i, "u1"), ACT.Square, scale=math.sqrt(2.0)),
             lambda i: tt(i, "u2", picked(i, pos_sb[2]), g(i, "m1"), ALU.subtract),
-            lambda i: turn(i, "Q", 3, g(i, "q1"), True, False),
+            lambda i: turn(i, "Q", 4, g(i, "q1"), True, False),
             lambda i: stt(i, "m2", g(i, "u2"), 1 / 3, g(i, "m1"), ALU.mult, ALU.add),
-            lambda i: act(i, "q2", g(i, "u2"), ACT.Square, scale=math.sqrt(1 / 6)),
+            lambda i: act(i, "q2", g(i, "u2"), ACT.Square, scale=math.sqrt(8 / 3)),
             lambda i: tt(i, "u3", picked(i, pos_sb[3]), g(i, "m2"), ALU.subtract),
-            lambda i: turn(i, "Q", 3, g(i, "q2"), False, False),
-            lambda i: act(i, "m4", g(i, "m2"), ACT.Copy, scale=4.0),
-            lambda i: act(i, "q3", g(i, "u3"), ACT.Square, scale=math.sqrt(3 / 16)),
-            lambda i: turn(i, "M", 5, g(i, "m4"), True, False),
-            lambda i: turn(i, "M", 5, g(i, "u3"), False, True),
-            lambda i: turn(i, "Q", 3, g(i, "q3"), False, True),
-            lambda i: nc.vector.tensor_copy(new(i, "yc"), picked(i, cen_sb)),
+            lambda i: turn(i, "Q", 4, g(i, "q2"), False, False),
+            lambda i: act(i, "q3", g(i, "u3"), ACT.Square, scale=math.sqrt(3.0)),
+            lambda i: stt(i, "nmu", g(i, "m2"), 4.0, g(i, "u3"), ALU.mult, ALU.add),
+            lambda i: (
+                turn(i, "Q", 4, g(i, "q3"), False, True),
+                turn(i, "G", 0, g(i, "nmu"), False, True),
+                turn(i, "M", 6, g(i, "nmu"), True, True),
+            ),
+            lambda i: nc.vector.tensor_copy(new(i, "yc", ("m20", "m21")[i]), picked(i, cen_sb)),
             lambda i: act(i, "rsd", g(i, "Q"), ACT.Abs_reciprocal_sqrt, bias=0.01),
-            lambda i: turn(i, "Y", 0, g(i, "yc"), True, True),
-            lambda i: stt(i, "hm", g(i, "M"), -0.25, hist_t[:, i, :], ALU.mult, ALU.add),
+            lambda i: turn(i, "Y", 2, g(i, "yc"), True, True),
+            lambda i: act(i, "ahm", g(i, "G"), ACT.Abs),
+            lambda i: act(i, "nsg", g(i, "G"), ACT.Sign, scale=-1.0, bias=-1e-30),
             lambda i: stt(i, "sd", g(i, "Q"), 0.01, g(i, "rsd"), ALU.add, ALU.mult),
-            lambda i: act(i, "ay", g(i, "Y"), ACT.Abs),
-            lambda i: tt(i, "t1", g(i, "hm"), g(i, "sd"), ALU.min),
+            lambda i: act(i, "ay", g(i, "Y"), ACT.Abs, scale=4.0),
+            lambda i: tt(i, "ms", g(i, "M"), g(i, "nsg"), ALU.mult),
+            lambda i: tt(i, "u", g(i, "ahm"), g(i, "sd"), ALU.min),
             lambda i: act(i, "wb", g(i, "ay"), ACT.Identity, scale=col(i, keep_s), bias=col(i, keep_s)),
-            lambda i: turn(i, "D", 3, col(i, abs_share).to_broadcast([P, P]), True, False),
-            lambda i: stt(i, "t2", g(i, "sd"), -1.0, g(i, "t1"), ALU.mult, ALU.max),
-            lambda i: turn(i, "D", 3, g(i, "wb"), False, False),
-            lambda i: stt(i, "cl", g(i, "M"), 0.25, g(i, "t2"), ALU.mult, ALU.add),
+            lambda i: turn(i, "D", 4, col(i, abs_share).to_broadcast([P, P]), True, False),
+            lambda i: tt(i, "cl", g(i, "u"), g(i, "ms"), ALU.add),
+            lambda i: turn(i, "D", 4, g(i, "wb"), False, False),
             lambda i: act(i, "ac", g(i, "cl"), ACT.Abs, scale=col(i, share)),
-            lambda i: tt(i, "n2", g(i, "wb"), g(i, "cl"), ALU.mult),
-            lambda i: turn(i, "D", 3, g(i, "ac"), False, True),
+            lambda i: stt(i, "bs", g(i, "wb"), 0.25, g(i, "nsg"), ALU.mult, ALU.mult),
+            lambda i: tt(i, "n2", g(i, "bs"), g(i, "cl"), ALU.mult),
+            lambda i: turn(i, "D", 4, g(i, "ac"), False, True),
             lambda i: stt(i, "n1", g(i, "ac"), col(i, abs_share), g(i, "Y"), ALU.add, ALU.mult),
-            lambda i: turn(i, "N", 5, g(i, "n2"), True, False),
+            lambda i: turn(i, "N", 6, g(i, "n2"), True, False),
             lambda i: act(i, "rd", g(i, "D"), ACT.Abs_reciprocal_sqrt),
             lambda i: act(i, "sg", g(i, "D"), ACT.Sign),
-            lambda i: turn(i, "N", 5, g(i, "n1"), False, True),
+            lambda i: turn(i, "N", 6, g(i, "n1"), False, True),
             lambda i: act(i, "rr", g(i, "rd"), ACT.Square),
-            lambda i: tt(i, "ns", g(i, "N"), g(i, "sg"), ALU.mult),
+            lambda i: stt(i, "ns", g(i, "N"), -4.0, g(i, "sg"), ALU.mult, ALU.mult),
             lambda i: tt(i, "res", g(i, "ns"), g(i, "rr"), ALU.mult),
             lambda i: nc.sync.dma_start(out[:, i * P : (i + 1) * P], g(i, "res")),
         ]
         for step in steps:
-            for i in range(len(pieces)):
+            for i in range(HALVES):
                 step(i)

@@ -20,10 +20,16 @@ ACT = mybir.ActivationFunctionType
 P = 128
 PACK = 4
 PASSES = K // (P * PACK)
-PER_COL = 16
-HALVES = V // P
+QUADRANT = 32
+SCALE_ROWS = 4
+PER_COLUMN = 16
 BLOCKS = S // P
-LAST_GATHERS = [[0,256],[256,384],[384,512]]
+HALVES = V // P
+VARIANCE_FLOOR = 0.01
+LAST_PASS_PIECES = ((0, 2), (2, 3), (3, 4))
+BANK_OFFSET, BANK_CENTRE = 0, 2
+BANK_VARIANCE, BANK_MEAN = 4, 6
+BANK_DEN, BANK_NUM = BANK_VARIANCE, BANK_MEAN
 
 
 def tile_picked_ytaa_lum_p_kernel(
@@ -34,56 +40,51 @@ def tile_picked_ytaa_lum_p_kernel(
         sb = ctx.enter_context(tc.tile_pool(name="sb", bufs=1))
         ps = ctx.enter_context(tc.psum_pool(name="ps", bufs=1))
 
-        def list_tile(name, src):
+        def load_list(name, src):
             tile = sb.tile([P, src.shape[1]], U16, name=name)
             nc.sync.dma_start(tile[:], src)
             return tile
 
+        def load_words(o):
+            tile = sb.tile([P, T], U32, name=f"word_table{o}", align_bytes=64)
+            nc.sync.dma_start(tile[:].bitcast(I32), x_words[o].rearrange("p n t -> p (n t)").bitcast(I32))
+            return tile
+
+        share = sb.tile([P, HALVES], F32, name="share")
+        with nc.allow_non_contiguous_dma(reason="one value of alpha a partition"):
+            nc.scalar.dma_start(share[:], alpha[0].rearrange("(h p) -> p h", p=P))
         scale_table = sb.tile([P, T], U8, name="scale_table", align_bytes=64)
         nc.vector.memset(scale_table[:].bitcast(I32), 0)
-        one_col = sb.tile([P, 1], F32, name="one_col")
-        nc.vector.memset(one_col[:], 1.0)
-        warm = sb.tile([P, 1], F32, name="warm")
-        nc.scalar.activation(warm[:], one_col[:], ACT.Abs_reciprocal_sqrt)
-
-        word_table = [sb.tile([P, T], U32, name=f"word_table{o}", align_bytes=64) for o in range(PASSES)]
-        w_raw = [sb.tile([P, PACK * N], F32, name=f"w_raw{o}") for o in range(PASSES)]
-        w_rows = w1.rearrange("(o p j) m -> o p (j m)", o=PASSES, j=PACK)
-
-        def load_words(o):
-            nc.sync.dma_start(word_table[o][:].bitcast(I32), x_words[o].rearrange("p n t -> p (n t)").bitcast(I32))
-
-        def load_scales():
-            for q in range(4):
-                nc.sync.dma_start(
-                    scale_table[32 * q : 32 * q + 4 * PASSES, :].bitcast(I32),
-                    x_scales[:, 4 * q : 4 * q + 4, :].bitcast(I32),
-                )
-
-        offs_sb = list_tile("offs_sb", offs)
-        load_words(0)
-        load_scales()
-        nc.sync.dma_start(w_raw[0][:], w_rows[0])
-        nc.sync.dma_start(w_raw[1][:], w_rows[1])
-        load_words(1)
-        share = sb.tile([P, HALVES], F32, name="share")
-        with nc.allow_non_contiguous_dma(reason="one share a partition"):
-            nc.sync.dma_start(share[:], alpha[0].rearrange("(h p) -> p h", p=P))
-        pos_sb = [list_tile(f"pos_sb{i}", src) for i, src in enumerate((pos1, pos2, pos3, pos4))]
-        cen_sb = list_tile("cen_sb", cen)
+        offs_sb = load_list("offs_sb", offs)
+        word_table = [load_words(0)]
+        for q in range(P // QUADRANT):
+            nc.sync.dma_start(
+                scale_table[QUADRANT * q : QUADRANT * q + PASSES * SCALE_ROWS, :].bitcast(I32),
+                x_scales[:, SCALE_ROWS * q : SCALE_ROWS * (q + 1), :].bitcast(I32),
+            )
+        w_raw = sb.tile([P, PASSES, PACK * N], F32, name="w_raw")
+        nc.sync.dma_start(w_raw[:], w1.rearrange("(o p t) m -> p o (t m)", o=PASSES, t=PACK))
+        word_table.append(load_words(1))
+        pos_sb = [load_list(f"pos_sb{d}", src) for d, src in enumerate((pos1, pos2, pos3, pos4))]
+        cen_sb = load_list("cen_sb", cen)
         hist_sb = sb.tile([P, V], F32, name="hist_sb")
         nc.sync.dma_start(hist_sb[:], hist)
+
+        one = sb.tile([P, 1], F32, name="one")
+        nc.vector.memset(one[:], 1.0)
+        warm = sb.tile([P, 1], F32, name="warm")
+        nc.scalar.activation(warm[:], one[:], ACT.Abs_reciprocal_sqrt)
         ident = sb.tile([P, P], F32, name="ident")
         make_identity(nc, ident[:])
 
-        sgn01 = sb.tile([P, HALVES], F32, name="sgn01")
-        nc.gpsimd.tensor_scalar(sgn01[:], share[:], 0.0, 2.0, ALU.is_ge, ALU.mult)
-        sgn = sb.tile([P, HALVES], F32, name="sgn")
-        nc.gpsimd.tensor_scalar(sgn[:], sgn01[:], 1.0, -1.0, ALU.mult, ALU.add)
-        abs_share = sb.tile([P, HALVES], F32, name="abs_share")
-        nc.gpsimd.tensor_tensor(abs_share[:], share[:], sgn[:], ALU.mult)
-        keep_s = sb.tile([P, HALVES], F32, name="keep_s")
-        nc.gpsimd.tensor_tensor(keep_s[:], sgn[:], abs_share[:], ALU.subtract)
+        share_abs = sb.tile([P, HALVES], F32, name="share_abs")
+        nc.vector.scalar_tensor_tensor(share_abs[:], share[:], -1.0, share[:], ALU.mult, ALU.max)
+        half_sign = sb.tile([P, HALVES], F32, name="half_sign")
+        nc.vector.tensor_scalar(half_sign[:], share[:], 0.0, 0.5, ALU.is_ge, ALU.subtract)
+        share_sign = sb.tile([P, HALVES], F32, name="share_sign")
+        nc.vector.tensor_scalar(share_sign[:], half_sign[:], 2.0, None, ALU.mult)
+        keep = sb.tile([P, HALVES], F32, name="keep")
+        nc.vector.scalar_tensor_tensor(keep[:], half_sign[:], 2.0, share_abs[:], ALU.mult, ALU.subtract)
 
         words = [sb.tile([P, S], U32, name=f"words{o}", align_bytes=64) for o in range(PASSES)]
         nc.vector.tensor_copy(words[0][:], word_table[0][:].indirect(offs_sb[:]))
@@ -93,118 +94,103 @@ def tile_picked_ytaa_lum_p_kernel(
         w_codes, w_scales = [], []
         for o in range(PASSES):
             w_bf = sb.tile([P, N, PACK], BF16, name=f"w_bf{o}", align_bytes=64)
-            nc.scalar.copy(w_bf[:], w_raw[o][:].rearrange("p (j m) -> p m j", j=PACK))
-            codes = sb.tile([P, N], U32, name=f"w_codes{o}", align_bytes=64)
-            plane = sb.tile([P, N], U8, name=f"w_scales{o}", align_bytes=64)
+            nc.scalar.copy(w_bf[:], w_raw[:, o, :].rearrange("p (t m) -> p m t", t=PACK))
+            w_codes.append(sb.tile([P, N], U32, name=f"w_codes{o}", align_bytes=64))
+            w_scales.append(sb.tile([P, N], U8, name=f"w_scales{o}", align_bytes=64))
             nc.vector.quantize_mx(
-                out=codes[:].bitcast(FP8X4), scales=plane[:], in_=w_bf[:].rearrange("p m j -> p (m j)")
+                out=w_codes[o][:].bitcast(FP8X4),
+                scales=w_scales[o][:],
+                in_=w_bf[:].rearrange("p m t -> p (m t)"),
             )
-            w_codes.append(codes)
-            w_scales.append(plane)
 
-        acc = [ps.tile([P, P], F32, name=f"acc{i}", tag=f"bank{i}") for i in range(BLOCKS)]
+        acc = [ps.tile([P, P], F32, name=f"acc{b}", tag=f"bank{b}") for b in range(BLOCKS)]
 
-        def product(o, i):
+        def product(o, b):
             nc.tensor.matmul_mx(
-                out=acc[i][:],
+                out=acc[b][:],
                 lhsT=w_codes[o][:].bitcast(FP8X4),
                 lhsT_scale=w_scales[o][:],
-                rhs=words[o][:, i * P : (i + 1) * P].bitcast(FP8X4),
-                rhs_scale=scales[4 * o : P, i * P : (i + 1) * P],
+                rhs=words[o][:, b * P : (b + 1) * P].bitcast(FP8X4),
+                rhs_scale=scales[SCALE_ROWS * o : P, b * P : (b + 1) * P],
                 start=(o == 0),
                 stop=(o == PASSES - 1),
             )
 
-        for i in range(BLOCKS):
-            product(0, i)
-        y = sb.tile([P, S], F32, name="y")
-        for a, b in LAST_GATHERS:
-            nc.vector.tensor_copy(
-                words[1][:, a:b], word_table[1][:].indirect(offs_sb[:, a // PER_COL : b // PER_COL])
-            )
-            for i in range(a // P, b // P):
-                product(1, i)
-        for i in range(BLOCKS):
-            if i == BLOCKS - 1:
-                nc.vector.tensor_scalar(y[:, i * P : (i + 1) * P], acc[i][:], -0.25, None, ALU.mult)
-            else:
-                nc.scalar.activation(y[:, i * P : (i + 1) * P], acc[i][:], ACT.Copy, scale=-0.25)
+        for b in range(BLOCKS):
+            product(0, b)
+        for first, end in LAST_PASS_PIECES:
+            entries = offs_sb[:, first * P // PER_COLUMN : end * P // PER_COLUMN]
+            nc.vector.tensor_copy(words[1][:, first * P : end * P], word_table[1][:].indirect(entries))
+            for b in range(first, end):
+                product(1, b)
 
-        t = [dict() for h in range(HALVES)]
+        neg_y = sb.tile([P, S], F32, name="neg_y")
+        for b in range(BLOCKS - 1):
+            nc.scalar.activation(neg_y[:, b * P : (b + 1) * P], acc[b][:], ACT.Copy, scale=-1.0)
+        nc.vector.tensor_scalar(neg_y[:, S - P :], acc[BLOCKS - 1][:], -1.0, None, ALU.mult)
 
-        def new(i, name, tag=None):
-            t[i][name] = sb.tile([P, P], F32, name=f"{name}{i}", tag=tag or f"{name}{i}")
-            return t[i][name][:]
+        val = [dict() for h in range(HALVES)]
 
-        def picked(i, lst):
-            return y[:].indirect(lst[:, i * P // PER_COL : (i + 1) * P // PER_COL])
+        def new(h, name, bytes_of=None):
+            val[h][name] = sb.tile([P, P], F32, name=f"{name}_{h}", tag=f"{bytes_of or name}_{h}")[:]
+            return val[h][name]
 
-        def tt(i, name, x, z, op):
-            nc.vector.tensor_tensor(new(i, name), x, z, op)
+        def picked(h, list_tile):
+            return neg_y[:].indirect(list_tile[:, h * P // PER_COLUMN : (h + 1) * P // PER_COLUMN])
 
-        def stt(i, name, x, scalar, z, op0, op1):
-            nc.vector.scalar_tensor_tensor(new(i, name), x, scalar, z, op0, op1)
+        def pair(h, name, in0, in1, op):
+            nc.vector.tensor_tensor(new(h, name), in0, in1, op)
 
-        def act(i, name, x, func, **kw):
-            nc.scalar.activation(new(i, name), x, func, **kw)
+        def scaled_pair(h, name, in0, scalar, op0, in1, op1):
+            nc.vector.scalar_tensor_tensor(new(h, name), in0, scalar, in1, op0, op1)
 
-        def g(i, name):
-            return t[i][name][:]
+        def single(h, name, in_, func, **affine):
+            nc.scalar.activation(new(h, name), in_, func, **affine)
 
-        def turn(i, name, bank, x, start, stop):
+        def turn(h, name, bank, in_, start, stop):
             if start:
-                t[i][name] = ps.tile([P, P], F32, name=f"{name}{i}", tag=f"bank{bank + i}")
-            nc.tensor.matmul(t[i][name][:], x, ident[:], start=start, stop=stop, is_transpose=True)
+                val[h][name] = ps.tile([P, P], F32, name=f"{name}_{h}", tag=f"bank{bank + h}")[:]
+            nc.tensor.matmul(val[h][name], in_, ident[:], start=start, stop=stop, is_transpose=True)
 
-        def col(i, tile):
-            return tile[:, i : i + 1]
+        for h, x in enumerate(val):
+            nc.vector.tensor_copy(new(h, "mean0"), picked(h, pos_sb[0]))
+            turn(h, "offset", BANK_OFFSET, hist_sb[:, h * P : (h + 1) * P], True, False)
+        for d, weight in ((1, 1 / 8), (2, 1 / 6), (3, 3 / 16)):
+            for h, x in enumerate(val):
+                pair(h, f"dev{d}", picked(h, pos_sb[d]), x[f"mean{d - 1}"], ALU.subtract)
+            for h, x in enumerate(val):
+                single(h, f"square{d}", x[f"dev{d}"], ACT.Square, scale=math.sqrt(weight))
+                scaled_pair(h, f"mean{d}", x[f"dev{d}"], 1 / (d + 1), ALU.mult, x[f"mean{d - 1}"], ALU.add)
+                turn(h, "variance", BANK_VARIANCE, x[f"square{d}"], d == 1, d == 3)
+        for h, x in enumerate(val):
+            turn(h, "offset", BANK_OFFSET, x["mean3"], False, True)
+            turn(h, "neg_mu", BANK_MEAN, x["mean3"], True, True)
+            nc.vector.tensor_copy(new(h, "neg_centre_plain", bytes_of="mean2"), picked(h, cen_sb))
+            turn(h, "neg_centre", BANK_CENTRE, x["neg_centre_plain"], True, True)
 
-        steps = [
-            lambda i: nc.vector.tensor_copy(new(i, "g0"), picked(i, pos_sb[0])),
-            lambda i: turn(i, "G", 0, hist_sb[:, i * P : (i + 1) * P], True, False),
-            lambda i: tt(i, "u1", picked(i, pos_sb[1]), g(i, "g0"), ALU.subtract),
-            lambda i: stt(i, "m1", g(i, "u1"), 0.5, g(i, "g0"), ALU.mult, ALU.add),
-            lambda i: act(i, "q1", g(i, "u1"), ACT.Square, scale=math.sqrt(2.0)),
-            lambda i: tt(i, "u2", picked(i, pos_sb[2]), g(i, "m1"), ALU.subtract),
-            lambda i: turn(i, "Q", 4, g(i, "q1"), True, False),
-            lambda i: stt(i, "m2", g(i, "u2"), 1 / 3, g(i, "m1"), ALU.mult, ALU.add),
-            lambda i: act(i, "q2", g(i, "u2"), ACT.Square, scale=math.sqrt(8 / 3)),
-            lambda i: tt(i, "u3", picked(i, pos_sb[3]), g(i, "m2"), ALU.subtract),
-            lambda i: turn(i, "Q", 4, g(i, "q2"), False, False),
-            lambda i: act(i, "q3", g(i, "u3"), ACT.Square, scale=math.sqrt(3.0)),
-            lambda i: stt(i, "nmu", g(i, "m2"), 4.0, g(i, "u3"), ALU.mult, ALU.add),
-            lambda i: (
-                turn(i, "Q", 4, g(i, "q3"), False, True),
-                turn(i, "G", 0, g(i, "nmu"), False, True),
-                turn(i, "M", 6, g(i, "nmu"), True, True),
-            ),
-            lambda i: nc.vector.tensor_copy(new(i, "yc", ("m20", "m21")[i]), picked(i, cen_sb)),
-            lambda i: act(i, "rsd", g(i, "Q"), ACT.Abs_reciprocal_sqrt, bias=0.01),
-            lambda i: turn(i, "Y", 2, g(i, "yc"), True, True),
-            lambda i: act(i, "ahm", g(i, "G"), ACT.Abs),
-            lambda i: act(i, "nsg", g(i, "G"), ACT.Sign, scale=-1.0, bias=-1e-30),
-            lambda i: stt(i, "sd", g(i, "Q"), 0.01, g(i, "rsd"), ALU.add, ALU.mult),
-            lambda i: act(i, "ay", g(i, "Y"), ACT.Abs, scale=4.0),
-            lambda i: tt(i, "ms", g(i, "M"), g(i, "nsg"), ALU.mult),
-            lambda i: tt(i, "u", g(i, "ahm"), g(i, "sd"), ALU.min),
-            lambda i: act(i, "wb", g(i, "ay"), ACT.Identity, scale=col(i, keep_s), bias=col(i, keep_s)),
-            lambda i: turn(i, "D", 4, col(i, abs_share).to_broadcast([P, P]), True, False),
-            lambda i: tt(i, "cl", g(i, "u"), g(i, "ms"), ALU.add),
-            lambda i: turn(i, "D", 4, g(i, "wb"), False, False),
-            lambda i: act(i, "ac", g(i, "cl"), ACT.Abs, scale=col(i, share)),
-            lambda i: stt(i, "bs", g(i, "wb"), 0.25, g(i, "nsg"), ALU.mult, ALU.mult),
-            lambda i: tt(i, "n2", g(i, "bs"), g(i, "cl"), ALU.mult),
-            lambda i: turn(i, "D", 4, g(i, "ac"), False, True),
-            lambda i: stt(i, "n1", g(i, "ac"), col(i, abs_share), g(i, "Y"), ALU.add, ALU.mult),
-            lambda i: turn(i, "N", 6, g(i, "n2"), True, False),
-            lambda i: act(i, "rd", g(i, "D"), ACT.Abs_reciprocal_sqrt),
-            lambda i: act(i, "sg", g(i, "D"), ACT.Sign),
-            lambda i: turn(i, "N", 6, g(i, "n1"), False, True),
-            lambda i: act(i, "rr", g(i, "rd"), ACT.Square),
-            lambda i: stt(i, "ns", g(i, "N"), -4.0, g(i, "sg"), ALU.mult, ALU.mult),
-            lambda i: tt(i, "res", g(i, "ns"), g(i, "rr"), ALU.mult),
-            lambda i: nc.sync.dma_start(out[:, i * P : (i + 1) * P], g(i, "res")),
-        ]
-        for step in steps:
-            for i in range(HALVES):
-                step(i)
+        for h, x in enumerate(val):
+            alpha_col, abs_col = share[:, h : h + 1], share_abs[:, h : h + 1]
+            sign_col, keep_col = share_sign[:, h : h + 1], keep[:, h : h + 1]
+            single(h, "inv_sd", x["variance"], ACT.Abs_reciprocal_sqrt, bias=VARIANCE_FLOOR)
+            scaled_pair(h, "sd", x["variance"], VARIANCE_FLOOR, ALU.add, x["inv_sd"], ALU.mult)
+            single(h, "distance", x["offset"], ACT.Abs)
+            single(h, "neg_side", x["offset"], ACT.Sign, scale=-1.0, bias=-1e-30)
+            pair(h, "side_mu", x["neg_mu"], x["neg_side"], ALU.mult)
+            pair(h, "step", x["distance"], x["sd"], ALU.min)
+            pair(h, "side_cl", x["step"], x["side_mu"], ALU.add)
+            single(h, "centre_abs", x["neg_centre"], ACT.Abs)
+            single(h, "den_centre", x["centre_abs"], ACT.Identity, scale=keep_col, bias=sign_col)
+            scaled_pair(h, "hist_weight", x["centre_abs"], 1.0, ALU.add, x["neg_side"], ALU.mult)
+            single(h, "den_clip", x["side_cl"], ACT.Abs, scale=alpha_col)
+            scaled_pair(h, "num_clip", x["side_cl"], keep_col, ALU.mult, x["hist_weight"], ALU.mult)
+            scaled_pair(h, "num_centre", x["den_clip"], abs_col, ALU.add, x["neg_centre"], ALU.mult)
+            turn(h, "den", BANK_DEN, x["den_centre"], True, False)
+            turn(h, "den", BANK_DEN, x["den_clip"], False, True)
+            turn(h, "neg_num", BANK_NUM, x["num_clip"], True, False)
+            turn(h, "neg_num", BANK_NUM, x["num_centre"], False, True)
+            single(h, "inv_root", x["den"], ACT.Abs_reciprocal_sqrt)
+            single(h, "den_sign", x["den"], ACT.Sign)
+            single(h, "inv_den", x["inv_root"], ACT.Square)
+            scaled_pair(h, "signed_num", x["neg_num"], -1.0, ALU.mult, x["den_sign"], ALU.mult)
+            pair(h, "result", x["signed_num"], x["inv_den"], ALU.mult)
+            nc.sync.dma_start(out[:, h * P : (h + 1) * P], x["result"])

@@ -1,4 +1,3 @@
-import math
 from contextlib import ExitStack
 
 import concourse.mybir as mybir
@@ -25,7 +24,9 @@ SCALE_ROWS = 4
 PER_COLUMN = 16
 BLOCKS = S // P
 HALVES = V // P
+NEIGHBOURS = 4
 VARIANCE_FLOOR = 0.01
+TIE_BREAK = 1e-30
 LAST_PASS_PIECES = ((0, 2), (2, 3), (3, 4))
 BANK_OFFSET, BANK_CENTRE = 0, 2
 BANK_VARIANCE, BANK_MEAN = 4, 6
@@ -50,9 +51,6 @@ def tile_picked_ytaa_lum_p_kernel(
             nc.sync.dma_start(tile[:].bitcast(I32), x_words[o].rearrange("p n t -> p (n t)").bitcast(I32))
             return tile
 
-        share = sb.tile([P, HALVES], F32, name="share")
-        with nc.allow_non_contiguous_dma(reason="one value of alpha a partition"):
-            nc.scalar.dma_start(share[:], alpha[0].rearrange("(h p) -> p h", p=P))
         scale_table = sb.tile([P, T], U8, name="scale_table", align_bytes=64)
         nc.vector.memset(scale_table[:].bitcast(I32), 0)
         offs_sb = load_list("offs_sb", offs)
@@ -62,18 +60,24 @@ def tile_picked_ytaa_lum_p_kernel(
                 scale_table[QUADRANT * q : QUADRANT * q + PASSES * SCALE_ROWS, :].bitcast(I32),
                 x_scales[:, SCALE_ROWS * q : SCALE_ROWS * (q + 1), :].bitcast(I32),
             )
-        w_raw = sb.tile([P, PASSES, PACK * N], F32, name="w_raw")
-        nc.sync.dma_start(w_raw[:], w1.rearrange("(o p t) m -> p o (t m)", o=PASSES, t=PACK))
+        w_rows = w1.rearrange("(o p t) m -> o p (t m)", o=PASSES, t=PACK)
+        w_raw = [sb.tile([P, PACK * N], F32, name=f"w_raw{o}") for o in range(PASSES)]
+        for o in range(PASSES):
+            nc.sync.dma_start(w_raw[o][:], w_rows[o])
         word_table.append(load_words(1))
         pos_sb = [load_list(f"pos_sb{d}", src) for d, src in enumerate((pos1, pos2, pos3, pos4))]
         cen_sb = load_list("cen_sb", cen)
         hist_sb = sb.tile([P, V], F32, name="hist_sb")
         nc.sync.dma_start(hist_sb[:], hist)
+        share = sb.tile([P, HALVES], F32, name="share")
+        with nc.allow_non_contiguous_dma(reason="one value of alpha a partition"):
+            nc.sync.dma_start(share[:], alpha[0].rearrange("(h p) -> p h", p=P))
 
         one = sb.tile([P, 1], F32, name="one")
         nc.vector.memset(one[:], 1.0)
-        warm = sb.tile([P, 1], F32, name="warm")
-        nc.scalar.activation(warm[:], one[:], ACT.Abs_reciprocal_sqrt)
+        root_weight = sb.tile([P, NEIGHBOURS - 1], F32, name="root_weight")
+        for d in range(1, NEIGHBOURS):
+            nc.scalar.activation(root_weight[:, d - 1 : d], one[:], ACT.Abs_reciprocal_sqrt, scale=4 + 4 / d)
         ident = sb.tile([P, P], F32, name="ident")
         make_identity(nc, ident[:])
 
@@ -94,7 +98,7 @@ def tile_picked_ytaa_lum_p_kernel(
         w_codes, w_scales = [], []
         for o in range(PASSES):
             w_bf = sb.tile([P, N, PACK], BF16, name=f"w_bf{o}", align_bytes=64)
-            nc.scalar.copy(w_bf[:], w_raw[:, o, :].rearrange("p (t m) -> p m t", t=PACK))
+            nc.scalar.copy(w_bf[:], w_raw[o][:].rearrange("p (t m) -> p m t", t=PACK))
             w_codes.append(sb.tile([P, N], U32, name=f"w_codes{o}", align_bytes=64))
             w_scales.append(sb.tile([P, N], U8, name=f"w_scales{o}", align_bytes=64))
             nc.vector.quantize_mx(
@@ -152,45 +156,45 @@ def tile_picked_ytaa_lum_p_kernel(
                 val[h][name] = ps.tile([P, P], F32, name=f"{name}_{h}", tag=f"bank{bank + h}")[:]
             nc.tensor.matmul(val[h][name], in_, ident[:], start=start, stop=stop, is_transpose=True)
 
-        for h, x in enumerate(val):
+        for h in range(HALVES):
             nc.vector.tensor_copy(new(h, "mean0"), picked(h, pos_sb[0]))
             turn(h, "offset", BANK_OFFSET, hist_sb[:, h * P : (h + 1) * P], True, False)
-        for d, weight in ((1, 1 / 8), (2, 1 / 6), (3, 3 / 16)):
-            for h, x in enumerate(val):
-                pair(h, f"dev{d}", picked(h, pos_sb[d]), x[f"mean{d - 1}"], ALU.subtract)
-            for h, x in enumerate(val):
-                single(h, f"square{d}", x[f"dev{d}"], ACT.Square, scale=math.sqrt(weight))
-                scaled_pair(h, f"mean{d}", x[f"dev{d}"], 1 / (d + 1), ALU.mult, x[f"mean{d - 1}"], ALU.add)
-                turn(h, "variance", BANK_VARIANCE, x[f"square{d}"], d == 1, d == 3)
-        for h, x in enumerate(val):
-            turn(h, "offset", BANK_OFFSET, x["mean3"], False, True)
-            turn(h, "neg_mu", BANK_MEAN, x["mean3"], True, True)
+        for d in range(1, NEIGHBOURS):
+            for h, here in enumerate(val):
+                pair(h, f"dev{d}", picked(h, pos_sb[d]), here[f"mean{d - 1}"], ALU.subtract)
+            for h, here in enumerate(val):
+                single(h, f"square{d}", here[f"dev{d}"], ACT.Square, scale=root_weight[:, d - 1 : d])
+                scaled_pair(h, f"mean{d}", here[f"dev{d}"], 1 / (d + 1), ALU.mult, here[f"mean{d - 1}"], ALU.add)
+                turn(h, "variance", BANK_VARIANCE, here[f"square{d}"], d == 1, d == NEIGHBOURS - 1)
+        for h, here in enumerate(val):
+            turn(h, "offset", BANK_OFFSET, here["mean3"], False, True)
+            turn(h, "neg_mu", BANK_MEAN, here["mean3"], True, True)
             nc.vector.tensor_copy(new(h, "neg_centre_plain", bytes_of="mean2"), picked(h, cen_sb))
-            turn(h, "neg_centre", BANK_CENTRE, x["neg_centre_plain"], True, True)
+            turn(h, "neg_centre", BANK_CENTRE, here["neg_centre_plain"], True, True)
 
-        for h, x in enumerate(val):
+        for h, here in enumerate(val):
             alpha_col, abs_col = share[:, h : h + 1], share_abs[:, h : h + 1]
             sign_col, keep_col = share_sign[:, h : h + 1], keep[:, h : h + 1]
-            single(h, "inv_sd", x["variance"], ACT.Abs_reciprocal_sqrt, bias=VARIANCE_FLOOR)
-            scaled_pair(h, "sd", x["variance"], VARIANCE_FLOOR, ALU.add, x["inv_sd"], ALU.mult)
-            single(h, "distance", x["offset"], ACT.Abs)
-            single(h, "neg_side", x["offset"], ACT.Sign, scale=-1.0, bias=-1e-30)
-            pair(h, "side_mu", x["neg_mu"], x["neg_side"], ALU.mult)
-            pair(h, "step", x["distance"], x["sd"], ALU.min)
-            pair(h, "side_cl", x["step"], x["side_mu"], ALU.add)
-            single(h, "centre_abs", x["neg_centre"], ACT.Abs)
-            single(h, "den_centre", x["centre_abs"], ACT.Identity, scale=keep_col, bias=sign_col)
-            scaled_pair(h, "hist_weight", x["centre_abs"], 1.0, ALU.add, x["neg_side"], ALU.mult)
-            single(h, "den_clip", x["side_cl"], ACT.Abs, scale=alpha_col)
-            scaled_pair(h, "num_clip", x["side_cl"], keep_col, ALU.mult, x["hist_weight"], ALU.mult)
-            scaled_pair(h, "num_centre", x["den_clip"], abs_col, ALU.add, x["neg_centre"], ALU.mult)
-            turn(h, "den", BANK_DEN, x["den_centre"], True, False)
-            turn(h, "den", BANK_DEN, x["den_clip"], False, True)
-            turn(h, "neg_num", BANK_NUM, x["num_clip"], True, False)
-            turn(h, "neg_num", BANK_NUM, x["num_centre"], False, True)
-            single(h, "inv_root", x["den"], ACT.Abs_reciprocal_sqrt)
-            single(h, "den_sign", x["den"], ACT.Sign)
-            single(h, "inv_den", x["inv_root"], ACT.Square)
-            scaled_pair(h, "signed_num", x["neg_num"], -1.0, ALU.mult, x["den_sign"], ALU.mult)
-            pair(h, "result", x["signed_num"], x["inv_den"], ALU.mult)
-            nc.sync.dma_start(out[:, h * P : (h + 1) * P], x["result"])
+            single(h, "inv_sd", here["variance"], ACT.Abs_reciprocal_sqrt, bias=VARIANCE_FLOOR)
+            scaled_pair(h, "sd", here["variance"], VARIANCE_FLOOR, ALU.add, here["inv_sd"], ALU.mult)
+            single(h, "distance", here["offset"], ACT.Abs)
+            single(h, "neg_side", here["offset"], ACT.Sign, scale=-1.0, bias=-TIE_BREAK)
+            pair(h, "side_mu", here["neg_mu"], here["neg_side"], ALU.mult)
+            pair(h, "step", here["distance"], here["sd"], ALU.min)
+            pair(h, "side_cl", here["step"], here["side_mu"], ALU.add)
+            single(h, "centre_abs", here["neg_centre"], ACT.Abs)
+            single(h, "den_centre", here["centre_abs"], ACT.Identity, scale=keep_col, bias=sign_col)
+            scaled_pair(h, "hist_weight", here["centre_abs"], 1.0, ALU.add, here["neg_side"], ALU.mult)
+            single(h, "den_clip", here["side_cl"], ACT.Abs, scale=alpha_col)
+            scaled_pair(h, "num_clip", here["side_cl"], keep_col, ALU.mult, here["hist_weight"], ALU.mult)
+            scaled_pair(h, "num_centre", here["den_clip"], abs_col, ALU.add, here["neg_centre"], ALU.mult)
+            turn(h, "den", BANK_DEN, here["den_centre"], True, False)
+            turn(h, "den", BANK_DEN, here["den_clip"], False, True)
+            turn(h, "neg_num", BANK_NUM, here["num_clip"], True, False)
+            turn(h, "neg_num", BANK_NUM, here["num_centre"], False, True)
+            single(h, "inv_root", here["den"], ACT.Abs_reciprocal_sqrt)
+            single(h, "den_sign", here["den"], ACT.Sign)
+            single(h, "inv_den", here["inv_root"], ACT.Square)
+            scaled_pair(h, "signed_num", here["neg_num"], -1.0, ALU.mult, here["den_sign"], ALU.mult)
+            pair(h, "result", here["signed_num"], here["inv_den"], ALU.mult)
+            nc.sync.dma_start(out[:, h * P : (h + 1) * P], here["result"])

from contextlib import ExitStack

import concourse.mybir as mybir
from concourse.masks import make_identity

K, T, S, N, V = 1024, 1024, 512, 128, 256
FLOPS = 2 * K * S * N

F32 = mybir.dt.float32
BF16 = mybir.dt.bfloat16
I32 = mybir.dt.int32
U32 = mybir.dt.uint32
U16 = mybir.dt.uint16
U8 = mybir.dt.uint8
FP8X4 = mybir.dt.float8_e4m3fn_x4
ALU = mybir.AluOpType
ACT = mybir.ActivationFunctionType

P = 128
PACK = 4
PASSES = K // (P * PACK)
QUADRANT = 32
SCALE_ROWS = 4
PER_COLUMN = 16
BLOCKS = S // P
HALVES = V // P
NEIGHBOURS = 4
VARIANCE_FLOOR = 0.01
TIE_BREAK = 1e-30
LAST_PASS_PIECES = ((0, 2), (2, 3), (3, 4))
BANK_OFFSET, BANK_CENTRE = 0, 2
BANK_VARIANCE, BANK_MEAN = 4, 6
BANK_DEN, BANK_NUM = BANK_VARIANCE, BANK_MEAN


def tile_picked_ytaa_lum_p_kernel(
    tc, x_words, x_scales, w1, hist, alpha, offs, pos1, pos2, pos3, pos4, cen, out
):
    nc = tc.nc
    with ExitStack() as ctx:
        sb = ctx.enter_context(tc.tile_pool(name="sb", bufs=1))
        ps = ctx.enter_context(tc.psum_pool(name="ps", bufs=1))

        def load_list(name, src):
            tile = sb.tile([P, src.shape[1]], U16, name=name)
            nc.sync.dma_start(tile[:], src)
            return tile

        def load_words(o):
            tile = sb.tile([P, T], U32, name=f"word_table{o}", align_bytes=64)
            nc.sync.dma_start(tile[:].bitcast(I32), x_words[o].rearrange("p n t -> p (n t)").bitcast(I32))
            return tile

        scale_table = sb.tile([P, T], U8, name="scale_table", align_bytes=64)
        nc.vector.memset(scale_table[:].bitcast(I32), 0)
        offs_sb = load_list("offs_sb", offs)
        word_table = [load_words(0)]
        for q in range(P // QUADRANT):
            nc.sync.dma_start(
                scale_table[QUADRANT * q : QUADRANT * q + PASSES * SCALE_ROWS, :].bitcast(I32),
                x_scales[:, SCALE_ROWS * q : SCALE_ROWS * (q + 1), :].bitcast(I32),
            )
        w_rows = w1.rearrange("(o p t) m -> o p (t m)", o=PASSES, t=PACK)
        w_raw = [sb.tile([P, PACK * N], F32, name=f"w_raw{o}") for o in range(PASSES)]
        for o in range(PASSES):
            nc.sync.dma_start(w_raw[o][:], w_rows[o])
        word_table.append(load_words(1))
        pos_sb = [load_list(f"pos_sb{d}", src) for d, src in enumerate((pos1, pos2, pos3, pos4))]
        cen_sb = load_list("cen_sb", cen)
        hist_sb = sb.tile([P, V], F32, name="hist_sb")
        nc.sync.dma_start(hist_sb[:], hist)
        share = sb.tile([P, HALVES], F32, name="share")
        with nc.allow_non_contiguous_dma(reason="one value of alpha a partition"):
            nc.sync.dma_start(share[:], alpha[0].rearrange("(h p) -> p h", p=P))

        one = sb.tile([P, 1], F32, name="one")
        nc.vector.memset(one[:], 1.0)
        root_weight = sb.tile([P, NEIGHBOURS - 1], F32, name="root_weight")
        for d in range(1, NEIGHBOURS):
            nc.scalar.activation(root_weight[:, d - 1 : d], one[:], ACT.Abs_reciprocal_sqrt, scale=4 + 4 / d)
        ident = sb.tile([P, P], F32, name="ident")
        make_identity(nc, ident[:])

        share_abs = sb.tile([P, HALVES], F32, name="share_abs")
        nc.vector.scalar_tensor_tensor(share_abs[:], share[:], -1.0, share[:], ALU.mult, ALU.max)
        half_sign = sb.tile([P, HALVES], F32, name="half_sign")
        nc.vector.tensor_scalar(half_sign[:], share[:], 0.0, 0.5, ALU.is_ge, ALU.subtract)
        share_sign = sb.tile([P, HALVES], F32, name="share_sign")
        nc.vector.tensor_scalar(share_sign[:], half_sign[:], 2.0, None, ALU.mult)
        keep = sb.tile([P, HALVES], F32, name="keep")
        nc.vector.scalar_tensor_tensor(keep[:], half_sign[:], 2.0, share_abs[:], ALU.mult, ALU.subtract)

        words = [sb.tile([P, S], U32, name=f"words{o}", align_bytes=64) for o in range(PASSES)]
        nc.vector.tensor_copy(words[0][:], word_table[0][:].indirect(offs_sb[:]))
        scales = sb.tile([P, S], U8, name="scales", align_bytes=64)
        nc.vector.tensor_copy(scales[:], scale_table[:].indirect(offs_sb[:]))

        w_codes, w_scales = [], []
        for o in range(PASSES):
            w_bf = sb.tile([P, N, PACK], BF16, name=f"w_bf{o}", align_bytes=64)
            nc.scalar.copy(w_bf[:], w_raw[o][:].rearrange("p (t m) -> p m t", t=PACK))
            w_codes.append(sb.tile([P, N], U32, name=f"w_codes{o}", align_bytes=64))
            w_scales.append(sb.tile([P, N], U8, name=f"w_scales{o}", align_bytes=64))
            nc.vector.quantize_mx(
                out=w_codes[o][:].bitcast(FP8X4),
                scales=w_scales[o][:],
                in_=w_bf[:].rearrange("p m t -> p (m t)"),
            )

        acc = [ps.tile([P, P], F32, name=f"acc{b}", tag=f"bank{b}") for b in range(BLOCKS)]

        def product(o, b):
            nc.tensor.matmul_mx(
                out=acc[b][:],
                lhsT=w_codes[o][:].bitcast(FP8X4),
                lhsT_scale=w_scales[o][:],
                rhs=words[o][:, b * P : (b + 1) * P].bitcast(FP8X4),
                rhs_scale=scales[SCALE_ROWS * o : P, b * P : (b + 1) * P],
                start=(o == 0),
                stop=(o == PASSES - 1),
            )

        for b in range(BLOCKS):
            product(0, b)
        for first, end in LAST_PASS_PIECES:
            entries = offs_sb[:, first * P // PER_COLUMN : end * P // PER_COLUMN]
            nc.vector.tensor_copy(words[1][:, first * P : end * P], word_table[1][:].indirect(entries))
            for b in range(first, end):
                product(1, b)

        neg_y = sb.tile([P, S], F32, name="neg_y")
        for b in range(BLOCKS - 1):
            nc.scalar.activation(neg_y[:, b * P : (b + 1) * P], acc[b][:], ACT.Copy, scale=-1.0)
        nc.vector.tensor_scalar(neg_y[:, S - P :], acc[BLOCKS - 1][:], -1.0, None, ALU.mult)

        val = [dict() for h in range(HALVES)]

        def new(h, name, bytes_of=None):
            val[h][name] = sb.tile([P, P], F32, name=f"{name}_{h}", tag=f"{bytes_of or name}_{h}")[:]
            return val[h][name]

        def picked(h, list_tile):
            return neg_y[:].indirect(list_tile[:, h * P // PER_COLUMN : (h + 1) * P // PER_COLUMN])

        def pair(h, name, in0, in1, op):
            nc.vector.tensor_tensor(new(h, name), in0, in1, op)

        def scaled_pair(h, name, in0, scalar, op0, in1, op1):
            nc.vector.scalar_tensor_tensor(new(h, name), in0, scalar, in1, op0, op1)

        def single(h, name, in_, func, **affine):
            nc.scalar.activation(new(h, name), in_, func, **affine)

        def turn(h, name, bank, in_, start, stop):
            if start:
                val[h][name] = ps.tile([P, P], F32, name=f"{name}_{h}", tag=f"bank{bank + h}")[:]
            nc.tensor.matmul(val[h][name], in_, ident[:], start=start, stop=stop, is_transpose=True)

        for h in range(HALVES):
            nc.vector.tensor_copy(new(h, "mean0"), picked(h, pos_sb[0]))
            turn(h, "offset", BANK_OFFSET, hist_sb[:, h * P : (h + 1) * P], True, False)
        for d in range(1, NEIGHBOURS):
            for h, here in enumerate(val):
                pair(h, f"dev{d}", picked(h, pos_sb[d]), here[f"mean{d - 1}"], ALU.subtract)
            for h, here in enumerate(val):
                single(h, f"square{d}", here[f"dev{d}"], ACT.Square, scale=root_weight[:, d - 1 : d])
                scaled_pair(h, f"mean{d}", here[f"dev{d}"], 1 / (d + 1), ALU.mult, here[f"mean{d - 1}"], ALU.add)
                turn(h, "variance", BANK_VARIANCE, here[f"square{d}"], d == 1, d == NEIGHBOURS - 1)
        for h, here in enumerate(val):
            turn(h, "offset", BANK_OFFSET, here["mean3"], False, True)
            turn(h, "neg_mu", BANK_MEAN, here["mean3"], True, True)
            nc.vector.tensor_copy(new(h, "neg_centre_plain", bytes_of="mean2"), picked(h, cen_sb))
            turn(h, "neg_centre", BANK_CENTRE, here["neg_centre_plain"], True, True)

        for h, here in enumerate(val):
            alpha_col, abs_col = share[:, h : h + 1], share_abs[:, h : h + 1]
            sign_col, keep_col = share_sign[:, h : h + 1], keep[:, h : h + 1]
            single(h, "inv_sd", here["variance"], ACT.Abs_reciprocal_sqrt, bias=VARIANCE_FLOOR)
            scaled_pair(h, "sd", here["variance"], VARIANCE_FLOOR, ALU.add, here["inv_sd"], ALU.mult)
            single(h, "distance", here["offset"], ACT.Abs)
            single(h, "neg_side", here["offset"], ACT.Sign, scale=-1.0, bias=-TIE_BREAK)
            pair(h, "side_mu", here["neg_mu"], here["neg_side"], ALU.mult)
            pair(h, "step", here["distance"], here["sd"], ALU.min)
            pair(h, "side_cl", here["step"], here["side_mu"], ALU.add)
            single(h, "centre_abs", here["neg_centre"], ACT.Abs)
            single(h, "den_centre", here["centre_abs"], ACT.Identity, scale=keep_col, bias=sign_col)
            scaled_pair(h, "hist_weight", here["centre_abs"], 1.0, ALU.add, here["neg_side"], ALU.mult)
            single(h, "den_clip", here["side_cl"], ACT.Abs, scale=alpha_col)
            scaled_pair(h, "num_clip", here["side_cl"], keep_col, ALU.mult, here["hist_weight"], ALU.mult)
            scaled_pair(h, "num_centre", here["den_clip"], abs_col, ALU.add, here["neg_centre"], ALU.mult)
            turn(h, "den", BANK_DEN, here["den_centre"], True, False)
            turn(h, "den", BANK_DEN, here["den_clip"], False, True)
            turn(h, "neg_num", BANK_NUM, here["num_clip"], True, False)
            turn(h, "neg_num", BANK_NUM, here["num_centre"], False, True)
            single(h, "inv_root", here["den"], ACT.Abs_reciprocal_sqrt)
            single(h, "den_sign", here["den"], ACT.Sign)
            single(h, "inv_den", here["inv_root"], ACT.Square)
            scaled_pair(h, "signed_num", here["neg_num"], -1.0, ALU.mult, here["den_sign"], ALU.mult)
            pair(h, "result", here["signed_num"], here["inv_den"], ALU.mult)
            nc.sync.dma_start(out[:, h * P : (h + 1) * P], here["result"])
